import numpy as np
import ml_dtypes


def mxq(x, axis, fmt="e4m3"):
    dtype, down = {"e4m3": (ml_dtypes.float8_e4m3fn, 7), "e5m2": (ml_dtypes.float8_e5m2, 14)}[fmt]
    v = np.moveaxis(np.asarray(x, np.float32).astype(ml_dtypes.bfloat16).astype(np.float64), axis, -1)
    blocks = v.reshape(v.shape[:-1] + (-1, 32))
    amax = np.abs(blocks).max(-1, keepdims=True)
    byte = np.maximum(np.where(amax > 0, np.frexp(amax)[1] - 1 + 127, 0) - down, 1)
    scale = np.exp2(byte - 127.0)
    codes = (blocks / scale).astype(np.float32).astype(dtype).astype(np.float64)
    return np.moveaxis((codes * scale).reshape(v.shape), -1, axis)


WIDE = False


def mx_kscale(k):
    if not WIDE:
        return np.ones(k)
    levels = np.array([10, -10, 5, -5, 0])
    if k % 512:
        return np.exp2(np.random.permutation(np.resize(levels, k // 32))).repeat(32)
    a = np.empty((k // 512, 16))
    for p in range(k // 512):
        a[p, :8] = np.random.permutation(np.resize(levels, 8))
        for g in range(8):
            far = levels[np.abs(levels - a[p, g]) >= 10]
            a[p, g + 8] = far[np.random.randint(len(far))]
    return np.exp2(a.ravel()).repeat(32)


def f64(x):
    return np.asarray(x).astype(np.float64)


def striped(idx):
    return np.tile(np.asarray(idx).reshape(-1, 16).T, (8, 1)).astype(np.uint16)


def unstriped(offs):
    return offs[:16].T.reshape(-1).astype(np.int64)


E2M1 = np.array([0.0, 0.5, 1.0, 1.5, 2.0, 3.0, 4.0, 6.0, -0.0, -0.5, -1.0, -1.5, -2.0, -3.0, -4.0, -6.0])


def pack_weight(w, fmt):
    k, n = w.shape
    w = f64(np.asarray(w, np.float32).astype(ml_dtypes.bfloat16)).reshape(k // 32, 32, n)
    amax = np.abs(w).max(1)
    if fmt == "e4m3":
        byte = np.frexp(amax)[1] - 1 + 127 - 7
    else:
        mant, ex = np.frexp(amax / 6.0)
        byte = np.where(mant > 0.5, ex, ex - 1) + 127
    byte = np.clip(np.where(amax > 0, byte, 1), 1, 254)
    scaled = (w * np.exp2(127.0 - byte)[:, None, :]).reshape(k, n).astype(np.float32)
    by_word = np.ascontiguousarray(scaled.reshape(k // 512, 128, 4, n).transpose(0, 1, 3, 2))
    if fmt == "e4m3":
        words = by_word.astype(ml_dtypes.float8_e4m3fn).view(np.uint8)
    else:
        c = by_word.astype(ml_dtypes.float4_e2m1fn).view(np.uint8) & 0xF
        words = (c[..., 0::2] | (c[..., 1::2] << 4)).reshape(k // 512, 128, 2 * n)
    return np.ascontiguousarray(words), np.ascontiguousarray(byte.astype(np.uint8).reshape(k // 512, 16, n))


def unpack_weight(words, scales, fmt):
    g, _, n = scales.shape
    words = np.ascontiguousarray(words).reshape(g, 128, n, -1)
    if fmt == "e4m3":
        vals = words.view(ml_dtypes.float8_e4m3fn).astype(np.float64)
    else:
        nib = np.empty((g, 128, n, 4), np.uint8)
        nib[..., 0::2] = words & 0xF
        nib[..., 1::2] = words >> 4
        vals = E2M1[nib]
    vals = vals * np.repeat(np.exp2(scales.astype(np.float64) - 127.0), 8, axis=1)[..., None]
    return vals.transpose(0, 1, 3, 2).reshape(g * 512, n)


def sigmoid(v):
    return 1.0 / (1.0 + np.exp(-v))


D, T, I, Q, Z, M = 512, 2048, 512, 128, 1024, 2048


def setup_inputs():
    n = np.random.standard_normal
    idx = np.random.permutation(T)[:I]
    idx2 = np.random.permutation(Z)[:I]
    idx3 = np.random.permutation(Z)[:I]
    idx4 = np.random.permutation(M)[:I]
    fd = mx_kscale(D)
    keysp = pack_weight(n((D, T)) / fd[:, None], "e4m3")
    return {
        "query": (n((D, Q)) * 1.0 / np.sqrt(D) * fd[:, None]).astype(np.float32),
        "keys_words": keysp[0],
        "keys_scales": keysp[1],
        "old": (np.random.uniform(0.0, 2.0, (Q, M))).astype(np.float32),
        "fade": (np.random.uniform(0.3, 0.9, (Q, 1))).astype(np.float32),
        "offs": striped(idx),
        "offs2": striped(idx2),
        "offs3": striped(idx3),
        "offs4": striped(idx4),
    }


def reference(query, keys_words, keys_scales, old, fade, offs, offs2, offs3, offs4):
    idx = unstriped(offs)
    idx2 = unstriped(offs2)
    idx3 = unstriped(offs3)
    idx4 = unstriped(offs4)
    keysu = unpack_weight(keys_words, keys_scales, "e4m3")
    queryq = mxq(f64(query), 0, "e4m3")
    keysidxg = keysu[:, idx]
    a = queryq.T @ keysidxg
    f0 = np.zeros((Q, Z))
    f0[:, idx2] = a
    s = a + f0[:, idx3]
    w = sigmoid(s)
    ws = w * 2.0
    wf = np.zeros((Q, M))
    wf[:, idx4] = ws
    y = f64(old) * f64(fade) + wf
    return y

@@ -1,0 +1,123 @@
+from contextlib import ExitStack
+
+import concourse.mybir as mybir
+
+D, T, I, Q, Z, M = 512, 2048, 512, 128, 1024, 2048
+FLOPS = 2 * D * I * Q
+
+F32 = mybir.dt.float32
+BF16 = mybir.dt.bfloat16
+I32 = mybir.dt.int32
+U32 = mybir.dt.uint32
+U16 = mybir.dt.uint16
+U8 = mybir.dt.uint8
+FP8X4 = mybir.dt.float8_e4m3fn_x4
+ACT = mybir.ActivationFunctionType
+ALU = mybir.AluOpType
+
+P = 128
+PACK = 4
+SLOT_RUNS = ((0, 128), (128, 256), (256, 512))
+PUT_RUNS = ((0, 128), (128, 512))
+OUT_RUNS = ((0, 256), (256, 768), (768, 1280), (1280, 1792), (1792, 2048))
+
+
+def entries(list_tile, first, last):
+    return list_tile[:, first // 16 : last // 16]
+
+
+def tile_attend_passedthrough_counts_lean_kernel(
+    tc, query, keys_words, keys_scales, old, fade, offs, offs2, offs3, offs4, out
+):
+    nc = tc.nc
+    with ExitStack() as ctx:
+        pool = ctx.enter_context(tc.tile_pool(name="pool", bufs=1))
+        psum = ctx.enter_context(tc.psum_pool(name="psum", bufs=1))
+
+        token_list = pool.tile([P, I // 16], U16)
+        put_list = pool.tile([P, I // 16], U16)
+        take_list = pool.tile([P, I // 16], U16)
+        column_list = pool.tile([P, I // 16], U16)
+        pool_words = pool.tile([P, T], I32, align_bytes=64)
+        pool_scales = pool.tile([P, T], U8, align_bytes=64, tag="packed")
+        query_rows = pool.tile([P, PACK, Q], F32, tag="staged")
+        places = pool.tile([P, Z], F32)
+        weights_put = pool.tile([P, M], F32)
+
+        nc.vector.memset(pool_scales[:].bitcast(I32), 0)
+        nc.scalar.dma_start(query_rows[:], query.rearrange("(p j) q -> p j q", j=PACK))
+        nc.scalar.dma_start(pool_words[:], keys_words[0].rearrange("p n t -> p (n t)").bitcast(I32))
+        nc.sync.dma_start(token_list[:], offs)
+        for quadrant in range(4):
+            nc.sync.dma_start(
+                pool_scales[32 * quadrant : 32 * quadrant + 4, :].bitcast(I32),
+                keys_scales[0, 4 * quadrant : 4 * quadrant + 4, :].bitcast(I32),
+            )
+        nc.sync.dma_start(put_list[:], offs2)
+        nc.sync.dma_start(take_list[:], offs3)
+        nc.sync.dma_start(column_list[:], offs4)
+        nc.vector.memset(places[:], 0.0)
+        nc.vector.memset(weights_put[:], 0.0)
+
+        query_bf = pool.tile([P, Q, PACK], BF16, align_bytes=64, tag="rounded")
+        nc.scalar.copy(query_bf[:], query_rows[:].rearrange("p j q -> p q j"))
+        fade_sb = pool.tile([P, 1], F32, tag="staged")
+        nc.sync.dma_start(fade_sb[:], fade)
+        slot_scales = pool.tile([P, I], U8, align_bytes=64)
+        nc.vector.tensor_copy(slot_scales[:], pool_scales[:].indirect(token_list[:]))
+        query_words = pool.tile([P, Q], U32, align_bytes=64)
+        query_scales = pool.tile([P, Q], U8, align_bytes=64)
+        nc.vector.quantize_mx(
+            out=query_words[:].bitcast(FP8X4),
+            scales=query_scales[:],
+            in_=query_bf[:].rearrange("p q j -> p (q j)"),
+        )
+
+        old_sb = pool.tile([P, M], F32, align_bytes=64, tag="rounded")
+        nc.sync.dma_start(old_sb[:], old)
+        slot_words = pool.tile([P, I], U32, align_bytes=64, tag="packed")
+        products = pool.tile([P, I], F32)
+        for run, (first, last) in enumerate(SLOT_RUNS):
+            nc.vector.tensor_copy(
+                slot_words[:, first:last], pool_words[:].bitcast(U32).indirect(entries(token_list, first, last))
+            )
+            bank = psum.tile([P, last - first], F32, name=f"bank{run}")
+            nc.tensor.matmul_mx(
+                out=bank[:],
+                lhsT=query_words[:].bitcast(FP8X4),
+                lhsT_scale=query_scales[:],
+                rhs=slot_words[:, first:last].bitcast(FP8X4),
+                rhs_scale=slot_scales[:, first:last],
+                start=True,
+                stop=True,
+            )
+            nc.scalar.copy(products[:, first:last], bank[:])
+
+        for first, last in PUT_RUNS:
+            nc.vector.tensor_copy(places[:].indirect(entries(put_list, first, last)), products[:, first:last])
+
+        scores = pool.tile([P, I], F32)
+        weights = pool.tile([P, I], F32)
+        for first, last in SLOT_RUNS:
+            nc.vector.tensor_tensor(
+                scores[:, first:last],
+                places[:].indirect(entries(take_list, first, last)),
+                products[:, first:last],
+                ALU.add,
+            )
+            nc.scalar.activation(weights[:, first:last], scores[:, first:last], ACT.Sigmoid)
+
+        for first, last in PUT_RUNS:
+            nc.vector.tensor_tensor(
+                weights_put[:].indirect(entries(column_list, first, last)),
+                weights[:, first:last],
+                weights[:, first:last],
+                ALU.add,
+            )
+
+        for run, (first, last) in enumerate(OUT_RUNS):
+            result = pool.tile([P, last - first], F32, name=f"result{run}")
+            nc.vector.scalar_tensor_tensor(
+                result[:], old_sb[:, first:last], fade_sb[:], weights_put[:, first:last], ALU.mult, ALU.add
+            )
+            nc.sync.dma_start(out[:, first:last], result[:])

@@ -17,9 +17,11 @@ ALU = mybir.AluOpType
 
 P = 128
 PACK = 4
-SLOT_RUNS = ((0, 128), (128, 256), (256, 512))
+SLOT_RUNS = ((0, 128), (128, 384), (384, 512))
+TAKE_RUNS = ((0, 128), (128, 320))
+SPLIT = 320
 PUT_RUNS = ((0, 128), (128, 512))
-OUT_RUNS = ((0, 256), (256, 768), (768, 1280), (1280, 1792), (1792, 2048))
+OUT_RUNS = ((0, 128), (128, 512), (512, 1024), (1024, 1536), (1536, 1920), (1920, 2048))
 
 
 def entries(list_tile, first, last):
@@ -42,22 +44,25 @@ def tile_attend_passedthrough_counts_lean_kernel(
         pool_scales = pool.tile([P, T], U8, align_bytes=64, tag="packed")
         query_rows = pool.tile([P, PACK, Q], F32, tag="staged")
         places = pool.tile([P, Z], F32)
-        weights_put = pool.tile([P, M], F32)
 
-        nc.vector.memset(pool_scales[:].bitcast(I32), 0)
-        nc.scalar.dma_start(query_rows[:], query.rearrange("(p j) q -> p j q", j=PACK))
-        nc.scalar.dma_start(pool_words[:], keys_words[0].rearrange("p n t -> p (n t)").bitcast(I32))
+        scale_rows = pool.tile([P, T // 4], I32)
         nc.sync.dma_start(token_list[:], offs)
         for quadrant in range(4):
-            nc.sync.dma_start(
-                pool_scales[32 * quadrant : 32 * quadrant + 4, :].bitcast(I32),
+            queue = nc.sync if quadrant % 2 == 0 else nc.scalar
+            queue.dma_start(
+                scale_rows[32 * quadrant : 32 * quadrant + 4, :],
                 keys_scales[0, 4 * quadrant : 4 * quadrant + 4, :].bitcast(I32),
             )
+        nc.scalar.dma_start(query_rows[:], query.rearrange("(p j) q -> p j q", j=PACK))
+        nc.sync.dma_start(pool_words[:], keys_words[0].rearrange("p n t -> p (n t)").bitcast(I32))
         nc.sync.dma_start(put_list[:], offs2)
         nc.sync.dma_start(take_list[:], offs3)
         nc.sync.dma_start(column_list[:], offs4)
+        nc.vector.memset(pool_scales[:].bitcast(I32), 0)
         nc.vector.memset(places[:], 0.0)
-        nc.vector.memset(weights_put[:], 0.0)
+        for quadrant in range(4):
+            rows = slice(32 * quadrant, 32 * quadrant + 4)
+            nc.vector.tensor_copy(pool_scales[rows, :].bitcast(I32), scale_rows[rows, :])
 
         query_bf = pool.tile([P, Q, PACK], BF16, align_bytes=64, tag="rounded")
         nc.scalar.copy(query_bf[:], query_rows[:].rearrange("p j q -> p q j"))
@@ -91,20 +96,31 @@ def tile_attend_passedthrough_counts_lean_kernel(
                 start=True,
                 stop=True,
             )
-            nc.scalar.copy(products[:, first:last], bank[:])
+            if run == 0:
+                nc.scalar.copy(products[:, first:last], bank[:])
+            else:
+                nc.vector.tensor_copy(products[:, first:last], bank[:])
 
+        weights_put = pool.tile([P, M], F32, align_bytes=64, tag="packed")
+        nc.vector.memset(weights_put[:], 0.0)
         for first, last in PUT_RUNS:
-            nc.vector.tensor_copy(places[:].indirect(entries(put_list, first, last)), products[:, first:last])
+            nc.scalar.activation(
+                places[:].indirect(entries(put_list, first, last)), products[:, first:last], ACT.Copy
+            )
 
         scores = pool.tile([P, I], F32)
         weights = pool.tile([P, I], F32)
-        for first, last in SLOT_RUNS:
+        taken = pool.tile([P, I - SPLIT], F32)
+        nc.scalar.activation(taken[:], places[:].indirect(entries(take_list, SPLIT, I)), ACT.Copy)
+        for first, last in TAKE_RUNS:
             nc.vector.tensor_tensor(
                 scores[:, first:last],
                 places[:].indirect(entries(take_list, first, last)),
                 products[:, first:last],
                 ALU.add,
             )
+        nc.vector.tensor_tensor(scores[:, SPLIT:], taken[:], products[:, SPLIT:], ALU.add)
+        for first, last in PUT_RUNS:
             nc.scalar.activation(weights[:, first:last], scores[:, first:last], ACT.Sigmoid)
 
         for first, last in PUT_RUNS:

@@ -65,6 +65,8 @@ def tile_attend_passedthrough_counts_lean_kernel(
             nc.vector.tensor_copy(pool_scales[rows, :].bitcast(I32), scale_rows[rows, :])
 
         query_bf = pool.tile([P, Q, PACK], BF16, align_bytes=64, tag="rounded")
+        warm = pool.tile([P, 1], F32)
+        nc.scalar.activation(warm[:], query_rows[:, 0, 0:1], ACT.Sigmoid)
         nc.scalar.copy(query_bf[:], query_rows[:].rearrange("p j q -> p q j"))
         fade_sb = pool.tile([P, 1], F32, tag="staged")
         nc.sync.dma_start(fade_sb[:], fade)

from contextlib import ExitStack

import concourse.mybir as mybir

D, T, I, Q, Z, M = 512, 2048, 512, 128, 1024, 2048
FLOPS = 2 * D * I * Q

F32 = mybir.dt.float32
BF16 = mybir.dt.bfloat16
I32 = mybir.dt.int32
U32 = mybir.dt.uint32
U16 = mybir.dt.uint16
U8 = mybir.dt.uint8
FP8X4 = mybir.dt.float8_e4m3fn_x4
ACT = mybir.ActivationFunctionType
ALU = mybir.AluOpType

P = 128
PACK = 4
SLOT_RUNS = ((0, 128), (128, 384), (384, 512))
TAKE_RUNS = ((0, 128), (128, 320))
SPLIT = 320
PUT_RUNS = ((0, 128), (128, 512))
OUT_RUNS = ((0, 128), (128, 512), (512, 1024), (1024, 1536), (1536, 1920), (1920, 2048))


def entries(list_tile, first, last):
    return list_tile[:, first // 16 : last // 16]


def tile_attend_passedthrough_counts_lean_kernel(
    tc, query, keys_words, keys_scales, old, fade, offs, offs2, offs3, offs4, out
):
    nc = tc.nc
    with ExitStack() as ctx:
        pool = ctx.enter_context(tc.tile_pool(name="pool", bufs=1))
        psum = ctx.enter_context(tc.psum_pool(name="psum", bufs=1))

        token_list = pool.tile([P, I // 16], U16)
        put_list = pool.tile([P, I // 16], U16)
        take_list = pool.tile([P, I // 16], U16)
        column_list = pool.tile([P, I // 16], U16)
        pool_words = pool.tile([P, T], I32, align_bytes=64)
        pool_scales = pool.tile([P, T], U8, align_bytes=64, tag="packed")
        query_rows = pool.tile([P, PACK, Q], F32, tag="staged")
        places = pool.tile([P, Z], F32)

        scale_rows = pool.tile([P, T // 4], I32)
        nc.sync.dma_start(token_list[:], offs)
        for quadrant in range(4):
            queue = nc.sync if quadrant % 2 == 0 else nc.scalar
            queue.dma_start(
                scale_rows[32 * quadrant : 32 * quadrant + 4, :],
                keys_scales[0, 4 * quadrant : 4 * quadrant + 4, :].bitcast(I32),
            )
        nc.scalar.dma_start(query_rows[:], query.rearrange("(p j) q -> p j q", j=PACK))
        nc.sync.dma_start(pool_words[:], keys_words[0].rearrange("p n t -> p (n t)").bitcast(I32))
        nc.sync.dma_start(put_list[:], offs2)
        nc.sync.dma_start(take_list[:], offs3)
        nc.sync.dma_start(column_list[:], offs4)
        nc.vector.memset(pool_scales[:].bitcast(I32), 0)
        nc.vector.memset(places[:], 0.0)
        for quadrant in range(4):
            rows = slice(32 * quadrant, 32 * quadrant + 4)
            nc.vector.tensor_copy(pool_scales[rows, :].bitcast(I32), scale_rows[rows, :])

        query_bf = pool.tile([P, Q, PACK], BF16, align_bytes=64, tag="rounded")
        warm = pool.tile([P, 1], F32)
        nc.scalar.activation(warm[:], query_rows[:, 0, 0:1], ACT.Sigmoid)
        nc.scalar.copy(query_bf[:], query_rows[:].rearrange("p j q -> p q j"))
        fade_sb = pool.tile([P, 1], F32, tag="staged")
        nc.sync.dma_start(fade_sb[:], fade)
        slot_scales = pool.tile([P, I], U8, align_bytes=64)
        nc.vector.tensor_copy(slot_scales[:], pool_scales[:].indirect(token_list[:]))
        query_words = pool.tile([P, Q], U32, align_bytes=64)
        query_scales = pool.tile([P, Q], U8, align_bytes=64)
        nc.vector.quantize_mx(
            out=query_words[:].bitcast(FP8X4),
            scales=query_scales[:],
            in_=query_bf[:].rearrange("p q j -> p (q j)"),
        )

        old_sb = pool.tile([P, M], F32, align_bytes=64, tag="rounded")
        nc.sync.dma_start(old_sb[:], old)
        slot_words = pool.tile([P, I], U32, align_bytes=64, tag="packed")
        products = pool.tile([P, I], F32)
        for run, (first, last) in enumerate(SLOT_RUNS):
            nc.vector.tensor_copy(
                slot_words[:, first:last], pool_words[:].bitcast(U32).indirect(entries(token_list, first, last))
            )
            bank = psum.tile([P, last - first], F32, name=f"bank{run}")
            nc.tensor.matmul_mx(
                out=bank[:],
                lhsT=query_words[:].bitcast(FP8X4),
                lhsT_scale=query_scales[:],
                rhs=slot_words[:, first:last].bitcast(FP8X4),
                rhs_scale=slot_scales[:, first:last],
                start=True,
                stop=True,
            )
            if run == 0:
                nc.scalar.copy(products[:, first:last], bank[:])
            else:
                nc.vector.tensor_copy(products[:, first:last], bank[:])

        weights_put = pool.tile([P, M], F32, align_bytes=64, tag="packed")
        nc.vector.memset(weights_put[:], 0.0)
        for first, last in PUT_RUNS:
            nc.scalar.activation(
                places[:].indirect(entries(put_list, first, last)), products[:, first:last], ACT.Copy
            )

        scores = pool.tile([P, I], F32)
        weights = pool.tile([P, I], F32)
        taken = pool.tile([P, I - SPLIT], F32)
        nc.scalar.activation(taken[:], places[:].indirect(entries(take_list, SPLIT, I)), ACT.Copy)
        for first, last in TAKE_RUNS:
            nc.vector.tensor_tensor(
                scores[:, first:last],
                places[:].indirect(entries(take_list, first, last)),
                products[:, first:last],
                ALU.add,
            )
        nc.vector.tensor_tensor(scores[:, SPLIT:], taken[:], products[:, SPLIT:], ALU.add)
        for first, last in PUT_RUNS:
            nc.scalar.activation(weights[:, first:last], scores[:, first:last], ACT.Sigmoid)

        for first, last in PUT_RUNS:
            nc.vector.tensor_tensor(
                weights_put[:].indirect(entries(column_list, first, last)),
                weights[:, first:last],
                weights[:, first:last],
                ALU.add,
            )

        for run, (first, last) in enumerate(OUT_RUNS):
            result = pool.tile([P, last - first], F32, name=f"result{run}")
            nc.vector.scalar_tensor_tensor(
                result[:], old_sb[:, first:last], fade_sb[:], weights_put[:, first:last], ALU.mult, ALU.add
            )
            nc.sync.dma_start(out[:, first:last], result[:])
